import numpy as np
import ml_dtypes


def mxq(x, axis, fmt="e4m3"):
    dtype, down = {"e4m3": (ml_dtypes.float8_e4m3fn, 7), "e5m2": (ml_dtypes.float8_e5m2, 14)}[fmt]
    v = np.moveaxis(np.asarray(x, np.float32).astype(ml_dtypes.bfloat16).astype(np.float64), axis, -1)
    blocks = v.reshape(v.shape[:-1] + (-1, 32))
    amax = np.abs(blocks).max(-1, keepdims=True)
    byte = np.maximum(np.where(amax > 0, np.frexp(amax)[1] - 1 + 127, 0) - down, 1)
    scale = np.exp2(byte - 127.0)
    codes = (blocks / scale).astype(np.float32).astype(dtype).astype(np.float64)
    return np.moveaxis((codes * scale).reshape(v.shape), -1, axis)


WIDE = False


def mx_kscale(k):
    if not WIDE:
        return np.ones(k)
    levels = np.array([10, -10, 5, -5, 0])
    if k % 512:
        return np.exp2(np.random.permutation(np.resize(levels, k // 32))).repeat(32)
    a = np.empty((k // 512, 16))
    for p in range(k // 512):
        a[p, :8] = np.random.permutation(np.resize(levels, 8))
        for g in range(8):
            far = levels[np.abs(levels - a[p, g]) >= 10]
            a[p, g + 8] = far[np.random.randint(len(far))]
    return np.exp2(a.ravel()).repeat(32)


def f64(x):
    return np.asarray(x).astype(np.float64)


def striped(idx):
    return np.tile(idx.reshape(-1, 16).T, (8, 1)).astype(np.uint16)


def unstriped(offs):
    return offs[:16].T.reshape(-1).astype(np.int64)


def pack_weight(w):
    k, n = w.shape
    w = f64(np.asarray(w, np.float32).astype(ml_dtypes.bfloat16)).reshape(k // 32, 32, n)
    amax = np.abs(w).max(1)
    byte = np.clip(np.where(amax > 0, np.frexp(amax)[1] - 1 + 127 - 7, 1), 1, 254)
    scaled = (w * np.exp2(127.0 - byte)[:, None, :]).reshape(k, n).astype(np.float32)
    words = np.ascontiguousarray(scaled.reshape(k // 512, 128, 4, n).transpose(0, 1, 3, 2)).astype(ml_dtypes.float8_e4m3fn).view(np.uint8)
    return words, np.ascontiguousarray(byte.astype(np.uint8).reshape(k // 512, 16, n))


def unpack_weight(words, scales):
    g, p, n, _ = words.shape
    vals = np.ascontiguousarray(words).view(ml_dtypes.float8_e4m3fn).astype(np.float64) * np.repeat(np.exp2(scales.astype(np.float64) - 127.0), 8, axis=1)[..., None]
    return vals.transpose(0, 1, 3, 2).reshape(g * 512, n)


E2M1 = np.array([0.0, 0.5, 1.0, 1.5, 2.0, 3.0, 4.0, 6.0, -0.0, -0.5, -1.0, -1.5, -2.0, -3.0, -4.0, -6.0])


def pack_fp4(w):
    k, n = w.shape
    w = f64(np.asarray(w, np.float32).astype(ml_dtypes.bfloat16)).reshape(k // 32, 32, n)
    amax = np.abs(w).max(1)
    mant, ex = np.frexp(amax / 6.0)
    byte = np.clip(np.where(amax > 0, np.where(mant > 0.5, ex, ex - 1) + 127, 1), 1, 254)
    scaled = (w * np.exp2(127.0 - byte)[:, None, :]).reshape(k, n).astype(np.float32)
    c = np.ascontiguousarray(scaled.reshape(k // 512, 128, 4, n).transpose(0, 1, 3, 2)).astype(ml_dtypes.float4_e2m1fn).view(np.uint8) & 0xF
    words = (c[..., 0::2] | (c[..., 1::2] << 4)).reshape(k // 512, 128, 2 * n)
    return np.ascontiguousarray(words), np.ascontiguousarray(byte.astype(np.uint8).reshape(k // 512, 16, n))


def unpack_fp4(words, scales):
    g, _, n = scales.shape
    words = np.ascontiguousarray(words).reshape(g, 128, n, 2)
    nib = np.empty((g, 128, n, 4), np.uint8)
    nib[..., 0::2] = words & 0xF
    nib[..., 1::2] = words >> 4
    vals = E2M1[nib] * np.repeat(np.exp2(scales.astype(np.float64) - 127.0), 8, axis=1)[..., None]
    return vals.transpose(0, 1, 3, 2).reshape(g * 512, n)


K, T, S, D, N, H, V, U = 512, 2048, 1024, 4, 256, 512, 256, 512


def setup_inputs():
    n = np.random.standard_normal
    s = mx_kscale(K)[:, None]
    u = mx_kscale(H)
    packed_xT = pack_weight(n((K, T)) * s)
    packed_w1 = pack_fp4(n((K, H)) / np.sqrt(K) / s)
    packed_w2 = pack_fp4(n((H, N)) / np.sqrt(H) / u[:, None])
    return {
        "x_words": packed_xT[0],
        "x_scales": packed_xT[1],
        "w1_words": packed_w1[0],
        "w1_scales": packed_w1[1],
        "unit": (np.random.uniform(0.6, 1.4, (H, 1)) * u[:, None]).astype(np.float32),
        "w2_words": packed_w2[0],
        "w2_scales": packed_w2[1],
        "offs": striped(np.random.permutation(T)[:S]),
        "lag": striped(np.random.permutation(S)),
        "note": striped(np.random.permutation(np.concatenate([np.arange(V), np.random.randint(0, V, U - V)]))),
    }


def reference(x_words, x_scales, w1_words, w1_scales, unit, w2_words, w2_scales, offs, lag, note):
    xq = unpack_weight(x_words, x_scales)[:, unstriped(offs)]
    y = unpack_fp4(w1_words, w1_scales).T @ xq
    yl = y[:, unstriped(lag)]
    dfn = (y - yl) ** 2
    cum = dfn.reshape(len(dfn), -1, D).mean(axis=2)
    cmnd = dfn / (np.repeat(cum, D, axis=1) + 0.3)
    best = cmnd.reshape(len(cmnd), -1, D).min(axis=2)
    mc = best[:, unstriped(note)] * (np.log(cum[:, unstriped(note)] + 0.2))
    hid = f64(unit) * mc
    return unpack_fp4(w2_words, w2_scales).T @ mxq(hid, 0, "e4m3")

@@ -1,0 +1,239 @@
+from contextlib import ExitStack
+
+import concourse.mybir as mybir
+from concourse.masks import make_identity
+
+K, T, S, D, N, H, V, U = 512, 2048, 1024, 4, 256, 512, 256, 512
+FLOPS = 2 * K * H * S + 2 * H * N * U
+
+F32 = mybir.dt.float32
+BF16 = mybir.dt.bfloat16
+I32 = mybir.dt.int32
+U32 = mybir.dt.uint32
+U16 = mybir.dt.uint16
+U8 = mybir.dt.uint8
+FP8X4 = mybir.dt.float8_e4m3fn_x4
+FP4X4 = mybir.dt.float4_e2m1fn_x4
+ACT = mybir.ActivationFunctionType
+ALU = mybir.AluOpType
+
+P = 128
+PACK = 4
+HALF = S // 2
+VH = V // 2
+UH = U // 2
+LAG_ON_SCALAR = ((1,0),(2,0))
+COPY_ON_VECTOR = ((1,0),(2,0))
+SUB_ON_GPSIMD = ((0, 0), (0, 1), (1, 0), (1, 1), (2, 0), (2, 1))
+SQ_ON_GPSIMD = ()
+NOTE_CHUNKS = (256,128,128)
+NOTE_ON_VECTOR = ((0,2),(0,3),(2,3))
+
+
+def load_scale_rows(nc, tile, rows):
+    for q in range(4):
+        nc.sync.dma_start(out=tile[32 * q : 32 * q + 32, :].bitcast(I32), in_=rows[4 * q : 4 * q + 4, :].bitcast(I32).partition_broadcast(8))
+
+
+def gather(nc, on_scalar, out, window, offsets):
+    if on_scalar:
+        nc.scalar.activation(out=out, in_=window.indirect(offsets), func=ACT.Copy)
+    else:
+        nc.vector.tensor_copy(out=out, in_=window.indirect(offsets))
+
+
+def tile_picked_yyinwd_log_p_kernel(
+    tc, x_words, x_scales, w1_words, w1_scales, unit, w2_words, w2_scales, offs, lag, note, out
+):
+    nc = tc.nc
+    with ExitStack() as ctx:
+        lists = ctx.enter_context(tc.tile_pool(name="lists", bufs=1))
+        keep = ctx.enter_context(tc.tile_pool(name="keep", bufs=1))
+        psum = ctx.enter_context(tc.psum_pool(name="psum", bufs=1))
+
+        offs_t = lists.tile([P, S // 16], U16, name="offs_t")
+        lag_t = lists.tile([P, S // 16], U16, name="lag_t")
+        note_t = lists.tile([P, U // 16], U16, name="note_t")
+
+        xw = keep.tile([P, T], U32, name="xw", align_bytes=64)
+        xs = keep.tile([P, T], U8, name="xs", align_bytes=64)
+        w1w_raw = keep.tile([P, 2 * H], U8, name="w1w_raw", align_bytes=64)
+        w1s_raw = keep.tile([P, H], U8, name="w1s_raw", align_bytes=64)
+        w1w = keep.tile([P, 2 * H], U8, name="w1w", align_bytes=64)
+        w1s = keep.tile([P, H], U8, name="w1s", align_bytes=64)
+        w2w = keep.tile([P, 2 * N], U8, name="w2w", align_bytes=64)
+        w2s = keep.tile([P, N], U8, name="w2s", align_bytes=64)
+        unit_t = keep.tile([P, PACK], F32, name="unit_t")
+        ident = keep.tile([P, P], F32, name="ident")
+
+        make_identity(nc, ident[:])
+        nc.sync.dma_start(offs_t[:], offs)
+        load_scale_rows(nc, xs, x_scales[0])
+        nc.sync.dma_start(out=xw[:].bitcast(I32), in_=x_words[0].rearrange("p n t -> p (n t)").bitcast(I32))
+        load_scale_rows(nc, w1s_raw, w1_scales[0])
+        nc.sync.dma_start(out=w1w_raw[:].bitcast(I32), in_=w1_words[0].bitcast(I32))
+        nc.sync.dma_start(lag_t[:], lag)
+        nc.sync.dma_start(note_t[:], note)
+        nc.sync.dma_start(out=unit_t[:], in_=unit.rearrange("(p t) o -> p (t o)", t=PACK))
+        nc.sync.dma_start(out=w2w[:].bitcast(I32), in_=w2_words[0].bitcast(I32))
+        load_scale_rows(nc, w2s, w2_scales[0])
+
+
+        nc.scalar.copy(
+            out=w1w[:].bitcast(U16).rearrange("p (t m) -> p t m", t=PACK),
+            in_=w1w_raw[:].bitcast(U16).rearrange("p (m t) -> p t m", t=PACK),
+        )
+        w1s_by_t = w1s_raw[:].rearrange("p (m t) -> p t m", t=PACK)
+        for t in range(PACK):
+            nc.gpsimd.tensor_copy(out=w1s[:, t * P : (t + 1) * P], in_=w1s_by_t[:, t, :])
+
+        xq_s = keep.tile([P, S], U8, name="xq_s", align_bytes=64)
+        nc.vector.tensor_copy(out=xq_s[:], in_=xs[:].indirect(offs_t[:]))
+        xq_w = {}
+        for h in range(2):
+            xq_w[h] = keep.tile([P, HALF], U32, name="xq_w%d" % h, align_bytes=64)
+            nc.vector.tensor_copy(out=xq_w[h][:], in_=xw[:].indirect(offs_t[:, 32 * h : 32 * h + 32]))
+        y_ps = {}
+        for t, h in ((0, 0), (1, 0), (0, 1), (2, 0), (1, 1), (3, 0), (2, 1), (3, 1)):
+            y_ps[t, h] = psum.tile([P, HALF], F32, name="y_ps%d%d" % (t, h), tag="bank%d" % (2 * t + h))
+            nc.tensor.matmul_mx(
+                out=y_ps[t, h][:],
+                lhsT=w1w[:, 2 * P * t : 2 * P * (t + 1)].bitcast(FP4X4),
+                lhsT_scale=w1s[:, P * t : P * (t + 1)],
+                rhs=xq_w[h][:].bitcast(FP8X4),
+                rhs_scale=xq_s[:, HALF * h : HALF * (h + 1)],
+                start=True,
+                stop=True,
+            )
+
+        ywin = [keep.tile([P, S], F32, name="ywin%d" % t) for t in range(PACK)]
+        sq = [keep.tile([P, S], F32, name="sq%d" % t) for t in range(PACK)]
+        logs_all = keep.tile([P, 2, 2 * V], F32, name="logs_all")
+        num = {}
+        m2 = {}
+        sums_ps = {}
+        logden_ps = {}
+
+        def empty_bank(t, h):
+            if (t, h) in COPY_ON_VECTOR:
+                nc.vector.tensor_copy(out=ywin[t][:, HALF * h : HALF * (h + 1)], in_=y_ps[t, h][:])
+            else:
+                nc.scalar.copy(out=ywin[t][:, HALF * h : HALF * (h + 1)], in_=y_ps[t, h][:])
+
+        yl = {}
+        diff = {}
+
+        def lagged(t, h):
+            yl[t, h] = keep.tile([P, HALF], F32, name="yl%d%d" % (t, h))
+            gather(nc, (t, h) in LAG_ON_SCALAR, yl[t, h][:], ywin[t][:], lag_t[:, 32 * h : 32 * h + 32])
+
+        def difference(t, h):
+            diff[t, h] = keep.tile([P, HALF], F32, name="diff%d%d" % (t, h), tag="diff%d%d" % (t % 2, h))
+            if (t, h) in SUB_ON_GPSIMD:
+                nc.gpsimd.tensor_tensor(out=diff[t, h][:], in0=ywin[t][:, HALF * h : HALF * (h + 1)], in1=yl[t, h][:], op=ALU.subtract)
+            else:
+                nc.vector.tensor_tensor(out=diff[t, h][:], in0=y_ps[t, h][:], in1=yl[t, h][:], op=ALU.subtract)
+
+        def square(t, h):
+            nc.scalar.activation(
+                out=sq[t][:, HALF * h : HALF * (h + 1)].rearrange("p (d v) -> p v d", d=D),
+                in_=diff[t, h][:].rearrange("p (v d) -> p v d", d=D),
+                func=ACT.Square,
+            )
+
+        def group_sums(t):
+            sums_ps[t] = psum.tile([P, 2 * V], F32, name="sums_ps%d" % t, tag="bank%d" % (2 * t))
+            for h in range(2):
+                for d in range(D):
+                    c0 = HALF * h + VH * d
+                    nc.tensor.matmul(
+                        out=sums_ps[t][:, VH * h : VH * (h + 1)],
+                        lhsT=sq[t][:, c0 : c0 + VH],
+                        rhs=ident[:],
+                        is_transpose=True,
+                        start=(d == 0),
+                        stop=(d == D - 1),
+                    )
+
+        def logarithms(t):
+            logs = logs_all[:, t % 2, :]
+            nc.scalar.activation(out=logs[:, V:], in_=sums_ps[t][:, :V], func=ACT.Ln, scale=1.0 / D, bias=0.3)
+            nc.scalar.activation(out=logs[:, :V], in_=sums_ps[t][:, :V], func=ACT.Ln, scale=1.0 / D, bias=0.2)
+            if t % 2 == 0:
+                logden_ps[t // 2] = psum.tile([P, 2 * V], F32, name="logden%d" % t, tag="bank%d" % (2 * t + 1))
+            for h in range(2):
+                c0 = V * (t % 2) + VH * h
+                nc.tensor.transpose(logden_ps[t // 2][:, c0 : c0 + VH], logs[:, V + VH * h : V + VH * (h + 1)], ident[:])
+            for h in range(2):
+                nc.tensor.transpose(sums_ps[t][:, V + VH * h : V + VH * (h + 1)], logs[:, VH * h : VH * (h + 1)], ident[:])
+
+        def minima(t):
+            m1 = keep.tile([P, 2, 2 * VH], F32, name="m1_%d" % t)
+            by_half = sq[t][:].rearrange("p (h c) -> p h c", h=2)
+            nc.vector.tensor_tensor(out=m1[:], in0=by_half[:, :, : 2 * VH], in1=by_half[:, :, 2 * VH :], op=ALU.min)
+            m2[t] = keep.tile([P, 2, VH], F32, name="m2_%d" % t)
+            nc.vector.tensor_tensor(out=m2[t][:], in0=m1[:, :, :VH], in1=m1[:, :, VH:], op=ALU.min)
+
+        def numerator(t):
+            num[t] = keep.tile([P, V], F32, name="num%d" % t)
+            nc.vector.scalar_tensor_tensor(
+                out=num[t][:],
+                in0=m2[t][:].rearrange("p h v -> p (h v)"),
+                scalar=unit_t[:, t : t + 1],
+                in1=sums_ps[t][:, V:],
+                op0=ALU.mult,
+                op1=ALU.mult,
+            )
+
+        for t, h in ((0, 0), (0, 1), (1, 0), (1, 1), (2, 0), (2, 1), (3, 0), (3, 1)):
+            empty_bank(t, h)
+        for t, h in ((0, 0), (0, 1), (1, 0), (1, 1), (2, 0), (2, 1), (3, 0), (3, 1)):
+            lagged(t, h)
+        for t, h in ((0, 0), (0, 1), (1, 0), (1, 1), (2, 0), (2, 1), (3, 0), (3, 1)):
+            difference(t, h)
+        for t in range(PACK):
+            square(t, 0)
+            square(t, 1)
+            group_sums(t)
+        for t in range(PACK):
+            logarithms(t)
+            minima(t)
+            numerator(t)
+
+        for t in range(PACK):
+            inv = logs_all[:, :, VH * t : VH * (t + 1)]
+            by_half = "p (h v) -> p h v"
+            nc.scalar.activation(
+                out=inv, in_=logden_ps[t // 2][:, V * (t % 2) : V * (t % 2 + 1)].rearrange(by_half, h=2), func=ACT.Exp, scale=-1.0
+            )
+            nc.vector.tensor_tensor(out=sq[t][:, :V].rearrange(by_half, h=2), in0=num[t][:].rearrange(by_half, h=2), in1=inv, op=ALU.mult)
+
+        out_banks = (3, 7, 0, 2, 4, 6, 1, 5)
+        r0 = 0
+        for g, width in enumerate(NOTE_CHUNKS):
+            planes = keep.tile([P, PACK, width], BF16, name="planes%d" % g, align_bytes=64)
+            for t in range(PACK):
+                gather(nc, (g, t) not in NOTE_ON_VECTOR, planes[:, t, :], sq[t][:], note_t[:, r0 // 16 : (r0 + width) // 16])
+            woven = keep.tile([P, width, PACK], BF16, name="woven%d" % g, align_bytes=64)
+            nc.vector.tensor_copy(out=woven[:], in_=planes[:].rearrange("p t r -> p r t"))
+            codes = keep.tile([P, width], U32, name="codes%d" % g, align_bytes=64)
+            scales = keep.tile([P, width], U8, name="scales%d" % g, align_bytes=64)
+            nc.vector.quantize_mx(out=codes[:].bitcast(FP8X4), scales=scales[:], in_=woven[:].rearrange("p r t -> p (r t)"))
+            for a in range(2):
+                o_ps = psum.tile([P, 2 * V], F32, name="o_ps%d%d" % (g, a), tag="bank%d" % out_banks[2 * g + a])
+                nc.tensor.matmul_mx(
+                    out=o_ps[:, :width],
+                    lhsT=w2w[:, 2 * P * a : 2 * P * (a + 1)].bitcast(FP4X4),
+                    lhsT_scale=w2s[:, P * a : P * (a + 1)],
+                    rhs=codes[:].bitcast(FP8X4),
+                    rhs_scale=scales[:],
+                    start=True,
+                    stop=True,
+                )
+                o_sb = keep.tile([P, width], F32, name="o_sb%d%d" % (g, a))
+                if a == 0 or g < 0:
+                    nc.scalar.copy(out=o_sb[:], in_=o_ps[:, :width])
+                else:
+                    nc.vector.tensor_copy(out=o_sb[:], in_=o_ps[:, :width])
+                nc.sync.dma_start(out=out[P * a : P * (a + 1), r0 : r0 + width], in_=o_sb[:])
+            r0 += width

@@ -22,12 +22,13 @@ PACK = 4
 HALF = S // 2
 VH = V // 2
 UH = U // 2
-LAG_ON_SCALAR = ((1,0),(2,0))
-COPY_ON_VECTOR = ((1,0),(2,0))
-SUB_ON_GPSIMD = ((0, 0), (0, 1), (1, 0), (1, 1), (2, 0), (2, 1))
-SQ_ON_GPSIMD = ()
-NOTE_CHUNKS = (256,128,128)
-NOTE_ON_VECTOR = ((0,2),(0,3),(2,3))
+PIECES = ((0, 256), (256, 768), (768, 1024))
+LAG_ON_SCALAR = ((1, 0), (1, 1), (3, 0), (3, 1))
+LAG_SHARED = (3, 0)
+COPY_ON_VECTOR = ((1, 1), (1, 2))
+NOTE_CHUNKS = (256, 128, 128)
+NOTE_ON_VECTOR = ((0, 2), (0, 3), (2, 3))
+OUT_ON_VECTOR = ((2, 1),)
 
 
 def load_scale_rows(nc, tile, rows):
@@ -40,6 +41,13 @@ def gather(nc, on_scalar, out, window, offsets):
         nc.scalar.activation(out=out, in_=window.indirect(offsets), func=ACT.Copy)
     else:
         nc.vector.tensor_copy(out=out, in_=window.indirect(offsets))
+
+
+def move(nc, on_vector, out, in_):
+    if on_vector:
+        nc.vector.tensor_copy(out=out, in_=in_)
+    else:
+        nc.scalar.copy(out=out, in_=in_)
 
 
 def tile_picked_yyinwd_log_p_kernel(
@@ -58,7 +66,7 @@ def tile_picked_yyinwd_log_p_kernel(
         xw = keep.tile([P, T], U32, name="xw", align_bytes=64)
         xs = keep.tile([P, T], U8, name="xs", align_bytes=64)
         w1w_raw = keep.tile([P, 2 * H], U8, name="w1w_raw", align_bytes=64)
-        w1s_raw = keep.tile([P, H], U8, name="w1s_raw", align_bytes=64)
+        w1s_raw = keep.tile([P, H], U8, name="w1s_raw", tag="w1s_raw", align_bytes=64)
         w1w = keep.tile([P, 2 * H], U8, name="w1w", align_bytes=64)
         w1s = keep.tile([P, H], U8, name="w1s", align_bytes=64)
         w2w = keep.tile([P, 2 * N], U8, name="w2w", align_bytes=64)
@@ -77,62 +85,82 @@ def tile_picked_yyinwd_log_p_kernel(
         nc.sync.dma_start(out=unit_t[:], in_=unit.rearrange("(p t) o -> p (t o)", t=PACK))
         nc.sync.dma_start(out=w2w[:].bitcast(I32), in_=w2_words[0].bitcast(I32))
         load_scale_rows(nc, w2s, w2_scales[0])
-
+        warm = keep.tile([P, 1], F32, name="warm")
+        nc.scalar.activation(out=warm[:], in_=ident[:, 0:1], func=ACT.Ln, bias=1.0)
 
         nc.scalar.copy(
             out=w1w[:].bitcast(U16).rearrange("p (t m) -> p t m", t=PACK),
             in_=w1w_raw[:].bitcast(U16).rearrange("p (m t) -> p t m", t=PACK),
         )
-        w1s_by_t = w1s_raw[:].rearrange("p (m t) -> p t m", t=PACK)
-        for t in range(PACK):
-            nc.gpsimd.tensor_copy(out=w1s[:, t * P : (t + 1) * P], in_=w1s_by_t[:, t, :])
+        nc.vector.tensor_copy(
+            out=w1s[:].rearrange("p (t m) -> p t m", t=PACK), in_=w1s_raw[:].rearrange("p (m t) -> p t m", t=PACK)
+        )
 
         xq_s = keep.tile([P, S], U8, name="xq_s", align_bytes=64)
         nc.vector.tensor_copy(out=xq_s[:], in_=xs[:].indirect(offs_t[:]))
-        xq_w = {}
-        for h in range(2):
-            xq_w[h] = keep.tile([P, HALF], U32, name="xq_w%d" % h, align_bytes=64)
-            nc.vector.tensor_copy(out=xq_w[h][:], in_=xw[:].indirect(offs_t[:, 32 * h : 32 * h + 32]))
+        ywin = [keep.tile([P, S], F32, name="ywin%d" % t) for t in range(PACK)]
+        sq = [keep.tile([P, S], F32, name="sq%d" % t) for t in range(PACK)]
+        xq_w = keep.tile([P, S], U32, name="xq_w", tag="w1s_raw", align_bytes=64)
+        for c0, c1 in PIECES:
+            nc.vector.tensor_copy(out=xq_w[:, c0:c1], in_=xw[:].indirect(offs_t[:, c0 // 16 : c1 // 16]))
+        banks = {}
         y_ps = {}
-        for t, h in ((0, 0), (1, 0), (0, 1), (2, 0), (1, 1), (3, 0), (2, 1), (3, 1)):
-            y_ps[t, h] = psum.tile([P, HALF], F32, name="y_ps%d%d" % (t, h), tag="bank%d" % (2 * t + h))
+
+        def product(t, k, bank, col):
+            c0, c1 = PIECES[k]
+            if bank not in banks:
+                banks[bank] = psum.tile([P, HALF], F32, name="y_ps%d" % bank, tag="bank%d" % bank)
+            y_ps[t, k] = banks[bank][:, col : col + c1 - c0]
             nc.tensor.matmul_mx(
-                out=y_ps[t, h][:],
+                out=y_ps[t, k],
                 lhsT=w1w[:, 2 * P * t : 2 * P * (t + 1)].bitcast(FP4X4),
                 lhsT_scale=w1s[:, P * t : P * (t + 1)],
-                rhs=xq_w[h][:].bitcast(FP8X4),
-                rhs_scale=xq_s[:, HALF * h : HALF * (h + 1)],
+                rhs=xq_w[:, c0:c1].bitcast(FP8X4),
+                rhs_scale=xq_s[:, c0:c1],
                 start=True,
                 stop=True,
             )
 
-        ywin = [keep.tile([P, S], F32, name="ywin%d" % t) for t in range(PACK)]
-        sq = [keep.tile([P, S], F32, name="sq%d" % t) for t in range(PACK)]
-        logs_all = keep.tile([P, 2, 2 * V], F32, name="logs_all")
+        def empty_bank(t, k):
+            c0, c1 = PIECES[k]
+            move(nc, (t, k) in COPY_ON_VECTOR, ywin[t][:, c0:c1], y_ps[t, k])
+
+        for t in range(PACK):
+            product(t, 0, t // 2, 256 * (t % 2))
+        product(0, 1, 2, 0)
+        product(1, 1, 3, 0)
+        product(0, 2, 6, 0)
+        product(1, 2, 7, 0)
+        for t in range(PACK):
+            empty_bank(t, 0)
+        for t in range(2):
+            empty_bank(t, 1)
+            empty_bank(t, 2)
+        for t in range(2, PACK):
+            product(t, 1, 2 + t, 0)
+            product(t, 2, 4 + t, 256)
+            empty_bank(t, 1)
+            empty_bank(t, 2)
+
+        logs_all = keep.tile([P, PACK, 2 * V], F32, name="logs_all")
         num = {}
         m2 = {}
         sums_ps = {}
         logden_ps = {}
-
-        def empty_bank(t, h):
-            if (t, h) in COPY_ON_VECTOR:
-                nc.vector.tensor_copy(out=ywin[t][:, HALF * h : HALF * (h + 1)], in_=y_ps[t, h][:])
-            else:
-                nc.scalar.copy(out=ywin[t][:, HALF * h : HALF * (h + 1)], in_=y_ps[t, h][:])
-
         yl = {}
         diff = {}
 
         def lagged(t, h):
             yl[t, h] = keep.tile([P, HALF], F32, name="yl%d%d" % (t, h))
-            gather(nc, (t, h) in LAG_ON_SCALAR, yl[t, h][:], ywin[t][:], lag_t[:, 32 * h : 32 * h + 32])
+            if (t, h) == LAG_SHARED:
+                for q in range(2):
+                    gather(nc, q == 1, yl[t, h][:, 256 * q : 256 * (q + 1)], ywin[t][:], lag_t[:, 32 * h + 16 * q : 32 * h + 16 * q + 16])
+            else:
+                gather(nc, (t, h) in LAG_ON_SCALAR, yl[t, h][:], ywin[t][:], lag_t[:, 32 * h : 32 * h + 32])
 
         def difference(t, h):
-            diff[t, h] = keep.tile([P, HALF], F32, name="diff%d%d" % (t, h), tag="diff%d%d" % (t % 2, h))
-            if (t, h) in SUB_ON_GPSIMD:
-                nc.gpsimd.tensor_tensor(out=diff[t, h][:], in0=ywin[t][:, HALF * h : HALF * (h + 1)], in1=yl[t, h][:], op=ALU.subtract)
-            else:
-                nc.vector.tensor_tensor(out=diff[t, h][:], in0=y_ps[t, h][:], in1=yl[t, h][:], op=ALU.subtract)
+            diff[t, h] = keep.tile([P, HALF], F32, name="diff%d%d" % (t, h), tag="diff%d%d" % (t, h))
+            nc.vector.tensor_tensor(out=diff[t, h][:], in0=ywin[t][:, HALF * h : HALF * (h + 1)], in1=yl[t, h][:], op=ALU.subtract)
 
         def square(t, h):
             nc.scalar.activation(
@@ -142,7 +170,7 @@ def tile_picked_yyinwd_log_p_kernel(
             )
 
         def group_sums(t):
-            sums_ps[t] = psum.tile([P, 2 * V], F32, name="sums_ps%d" % t, tag="bank%d" % (2 * t))
+            sums_ps[t] = psum.tile([P, 2 * V], F32, name="sums_ps%d" % t, tag="bank%d" % t)
             for h in range(2):
                 for d in range(D):
                     c0 = HALF * h + VH * d
@@ -156,11 +184,11 @@ def tile_picked_yyinwd_log_p_kernel(
                     )
 
         def logarithms(t):
-            logs = logs_all[:, t % 2, :]
+            logs = logs_all[:, t, :]
             nc.scalar.activation(out=logs[:, V:], in_=sums_ps[t][:, :V], func=ACT.Ln, scale=1.0 / D, bias=0.3)
             nc.scalar.activation(out=logs[:, :V], in_=sums_ps[t][:, :V], func=ACT.Ln, scale=1.0 / D, bias=0.2)
             if t % 2 == 0:
-                logden_ps[t // 2] = psum.tile([P, 2 * V], F32, name="logden%d" % t, tag="bank%d" % (2 * t + 1))
+                logden_ps[t // 2] = psum.tile([P, 2 * V], F32, name="logden%d" % t, tag="bank%d" % (4 + t // 2))
             for h in range(2):
                 c0 = V * (t % 2) + VH * h
                 nc.tensor.transpose(logden_ps[t // 2][:, c0 : c0 + VH], logs[:, V + VH * h : V + VH * (h + 1)], ident[:])
@@ -186,8 +214,6 @@ def tile_picked_yyinwd_log_p_kernel(
             )
 
         for t, h in ((0, 0), (0, 1), (1, 0), (1, 1), (2, 0), (2, 1), (3, 0), (3, 1)):
-            empty_bank(t, h)
-        for t, h in ((0, 0), (0, 1), (1, 0), (1, 1), (2, 0), (2, 1), (3, 0), (3, 1)):
             lagged(t, h)
         for t, h in ((0, 0), (0, 1), (1, 0), (1, 1), (2, 0), (2, 1), (3, 0), (3, 1)):
             difference(t, h)
@@ -197,18 +223,19 @@ def tile_picked_yyinwd_log_p_kernel(
             group_sums(t)
         for t in range(PACK):
             logarithms(t)
+        for t in range(PACK):
             minima(t)
             numerator(t)
 
         for t in range(PACK):
-            inv = logs_all[:, :, VH * t : VH * (t + 1)]
+            inv = logs_all[:, 2:, VH * t : VH * (t + 1)]
             by_half = "p (h v) -> p h v"
             nc.scalar.activation(
                 out=inv, in_=logden_ps[t // 2][:, V * (t % 2) : V * (t % 2 + 1)].rearrange(by_half, h=2), func=ACT.Exp, scale=-1.0
             )
             nc.vector.tensor_tensor(out=sq[t][:, :V].rearrange(by_half, h=2), in0=num[t][:].rearrange(by_half, h=2), in1=inv, op=ALU.mult)
 
-        out_banks = (3, 7, 0, 2, 4, 6, 1, 5)
+        out_banks = (6, 7, 0, 1, 2, 3, 4, 5)
         r0 = 0
         for g, width in enumerate(NOTE_CHUNKS):
             planes = keep.tile([P, PACK, width], BF16, name="planes%d" % g, align_bytes=64)
@@ -231,9 +258,6 @@ def tile_picked_yyinwd_log_p_kernel(
                     stop=True,
                 )
                 o_sb = keep.tile([P, width], F32, name="o_sb%d%d" % (g, a))
-                if a == 0 or g < 0:
-                    nc.scalar.copy(out=o_sb[:], in_=o_ps[:, :width])
-                else:
-                    nc.vector.tensor_copy(out=o_sb[:], in_=o_ps[:, :width])
+                move(nc, (g, a) in OUT_ON_VECTOR, o_sb[:], o_ps[:, :width])
                 nc.sync.dma_start(out=out[P * a : P * (a + 1), r0 : r0 + width], in_=o_sb[:])
             r0 += width

@@ -19,28 +19,34 @@ ALU = mybir.AluOpType
 
 P = 128
 PACK = 4
+PER_COLUMN = 16
+BANK = 512
 HALF = S // 2
-VH = V // 2
-UH = U // 2
-PIECES = ((0, 256), (256, 768), (768, 1024))
-LAG_ON_SCALAR = ((1, 0), (1, 1), (3, 0), (3, 1))
-LAG_SHARED = (3, 0)
-COPY_ON_VECTOR = ((1, 1), (1, 2))
-NOTE_CHUNKS = (256, 128, 128)
-NOTE_ON_VECTOR = ((0, 2), (0, 3), (2, 3))
-OUT_ON_VECTOR = ((2, 1),)
+GROUPS = HALF // D
+LAST = PACK - 1
+
+SHORT = 256
+PIECES = ((0, SHORT), (SHORT, S - SHORT), (S - SHORT, S))
+CHUNKS = ((0, 256), (256, 384), (384, U))
 
 
 def load_scale_rows(nc, tile, rows):
     for q in range(4):
-        nc.sync.dma_start(out=tile[32 * q : 32 * q + 32, :].bitcast(I32), in_=rows[4 * q : 4 * q + 4, :].bitcast(I32).partition_broadcast(8))
+        nc.sync.dma_start(
+            out=tile[32 * q : 32 * q + 32, :].bitcast(I32),
+            in_=rows[4 * q : 4 * q + 4, :].bitcast(I32).partition_broadcast(8),
+        )
 
 
-def gather(nc, on_scalar, out, window, offsets):
-    if on_scalar:
-        nc.scalar.activation(out=out, in_=window.indirect(offsets), func=ACT.Copy)
-    else:
+def entries(list_tile, first, end):
+    return list_tile[:, first // PER_COLUMN : end // PER_COLUMN]
+
+
+def gather(nc, on_vector, out, window, offsets):
+    if on_vector:
         nc.vector.tensor_copy(out=out, in_=window.indirect(offsets))
+    else:
+        nc.scalar.activation(out=out, in_=window.indirect(offsets), func=ACT.Copy)
 
 
 def move(nc, on_vector, out, in_):
@@ -59,14 +65,17 @@ def tile_picked_yyinwd_log_p_kernel(
         keep = ctx.enter_context(tc.tile_pool(name="keep", bufs=1))
         psum = ctx.enter_context(tc.psum_pool(name="psum", bufs=1))
 
-        offs_t = lists.tile([P, S // 16], U16, name="offs_t")
-        lag_t = lists.tile([P, S // 16], U16, name="lag_t")
-        note_t = lists.tile([P, U // 16], U16, name="note_t")
+        def bank_tile(name, bank):
+            return psum.tile([P, BANK], F32, name=name, tag="bank%d" % bank)
+
+        offs_t = lists.tile([P, S // PER_COLUMN], U16, name="offs_t")
+        lag_t = lists.tile([P, S // PER_COLUMN], U16, name="lag_t")
+        note_t = lists.tile([P, U // PER_COLUMN], U16, name="note_t")
 
         xw = keep.tile([P, T], U32, name="xw", align_bytes=64)
         xs = keep.tile([P, T], U8, name="xs", align_bytes=64)
         w1w_raw = keep.tile([P, 2 * H], U8, name="w1w_raw", align_bytes=64)
-        w1s_raw = keep.tile([P, H], U8, name="w1s_raw", tag="w1s_raw", align_bytes=64)
+        w1s_raw = keep.tile([P, H], U8, name="w1s_raw", tag="w1s_then_words", align_bytes=64)
         w1w = keep.tile([P, 2 * H], U8, name="w1w", align_bytes=64)
         w1s = keep.tile([P, H], U8, name="w1s", align_bytes=64)
         w2w = keep.tile([P, 2 * N], U8, name="w2w", align_bytes=64)
@@ -85,8 +94,11 @@ def tile_picked_yyinwd_log_p_kernel(
         nc.sync.dma_start(out=unit_t[:], in_=unit.rearrange("(p t) o -> p (t o)", t=PACK))
         nc.sync.dma_start(out=w2w[:].bitcast(I32), in_=w2_words[0].bitcast(I32))
         load_scale_rows(nc, w2s, w2_scales[0])
-        warm = keep.tile([P, 1], F32, name="warm")
-        nc.scalar.activation(out=warm[:], in_=ident[:, 0:1], func=ACT.Ln, bias=1.0)
+
+        one = keep.tile([P, 1], F32, name="one")
+        log_tenth = keep.tile([P, 1], F32, name="log_tenth")
+        nc.vector.memset(one[:], 1.0)
+        nc.scalar.activation(out=log_tenth[:], in_=one[:], func=ACT.Ln, scale=0.1)
 
         nc.scalar.copy(
             out=w1w[:].bitcast(U16).rearrange("p (t m) -> p t m", t=PACK),
@@ -98,19 +110,18 @@ def tile_picked_yyinwd_log_p_kernel(
 
         xq_s = keep.tile([P, S], U8, name="xq_s", align_bytes=64)
         nc.vector.tensor_copy(out=xq_s[:], in_=xs[:].indirect(offs_t[:]))
-        ywin = [keep.tile([P, S], F32, name="ywin%d" % t) for t in range(PACK)]
-        sq = [keep.tile([P, S], F32, name="sq%d" % t) for t in range(PACK)]
-        xq_w = keep.tile([P, S], U32, name="xq_w", tag="w1s_raw", align_bytes=64)
+        xq_w = keep.tile([P, S], U32, name="xq_w", tag="w1s_then_words", align_bytes=64)
         for c0, c1 in PIECES:
-            nc.vector.tensor_copy(out=xq_w[:, c0:c1], in_=xw[:].indirect(offs_t[:, c0 // 16 : c1 // 16]))
-        banks = {}
+            nc.vector.tensor_copy(out=xq_w[:, c0:c1], in_=xw[:].indirect(entries(offs_t, c0, c1)))
+
+        y = [keep.tile([P, S], F32, name="y%d" % t) for t in range(PACK)]
+        sq = [keep.tile([P, S], F32, name="sq%d" % t) for t in range(PACK)]
+        y_banks = [bank_tile("y_bank%d" % b, b) for b in range(8)]
         y_ps = {}
 
-        def product(t, k, bank, col):
+        def product(t, k, bank, column):
             c0, c1 = PIECES[k]
-            if bank not in banks:
-                banks[bank] = psum.tile([P, HALF], F32, name="y_ps%d" % bank, tag="bank%d" % bank)
-            y_ps[t, k] = banks[bank][:, col : col + c1 - c0]
+            y_ps[t, k] = y_banks[bank][:, column : column + c1 - c0]
             nc.tensor.matmul_mx(
                 out=y_ps[t, k],
                 lhsT=w1w[:, 2 * P * t : 2 * P * (t + 1)].bitcast(FP4X4),
@@ -123,14 +134,13 @@ def tile_picked_yyinwd_log_p_kernel(
 
         def empty_bank(t, k):
             c0, c1 = PIECES[k]
-            move(nc, (t, k) in COPY_ON_VECTOR, ywin[t][:, c0:c1], y_ps[t, k])
+            move(nc, t == 1 and k > 0, y[t][:, c0:c1], y_ps[t, k])
 
         for t in range(PACK):
-            product(t, 0, t // 2, 256 * (t % 2))
-        product(0, 1, 2, 0)
-        product(1, 1, 3, 0)
-        product(0, 2, 6, 0)
-        product(1, 2, 7, 0)
+            product(t, 0, t // 2, SHORT * (t % 2))
+        for k, first_bank in ((1, 2), (2, 6)):
+            for t in range(2):
+                product(t, k, first_bank + t, 0)
         for t in range(PACK):
             empty_bank(t, 0)
         for t in range(2):
@@ -138,29 +148,40 @@ def tile_picked_yyinwd_log_p_kernel(
             empty_bank(t, 2)
         for t in range(2, PACK):
             product(t, 1, 2 + t, 0)
-            product(t, 2, 4 + t, 256)
+            product(t, 2, 4 + t, SHORT)
             empty_bank(t, 1)
             empty_bank(t, 2)
 
-        logs_all = keep.tile([P, PACK, 2 * V], F32, name="logs_all")
-        num = {}
-        m2 = {}
-        sums_ps = {}
-        logden_ps = {}
-        yl = {}
+        logs_turned = keep.tile([P, PACK * V], F32, name="logs_turned")
+        inv = keep.tile([P, PACK * V], F32, name="inv")
+        log_bias = inv[:, 0:1]
+        log_scale = inv[:, V : V + 1]
+        nc.vector.tensor_scalar(out=log_bias, in0=ident[:, 0:1], scalar1=0.0, scalar2=0.2, op0=ALU.mult, op1=ALU.add)
+        nc.vector.memset(log_scale, 1.0 / D)
+        unit10 = keep.tile([P, PACK], F32, name="unit10")
+        nc.vector.tensor_scalar(out=unit10[:], in0=unit_t[:], scalar1=10.0, scalar2=None, op0=ALU.mult)
+
+        y_lag = {}
         diff = {}
+        sums_ps = {}
+        log_ps = {}
+        least = {}
+        num = {}
 
         def lagged(t, h):
-            yl[t, h] = keep.tile([P, HALF], F32, name="yl%d%d" % (t, h))
-            if (t, h) == LAG_SHARED:
-                for q in range(2):
-                    gather(nc, q == 1, yl[t, h][:, 256 * q : 256 * (q + 1)], ywin[t][:], lag_t[:, 32 * h + 16 * q : 32 * h + 16 * q + 16])
+            y_lag[t, h] = keep.tile([P, HALF], F32, name="y_lag%d%d" % (t, h))
+            if (t, h) == (LAST, 1):
+                for c0 in (0, HALF // 2):
+                    c1 = c0 + HALF // 2
+                    gather(nc, c0 == 0, y_lag[t, h][:, c0:c1], y[t][:], entries(lag_t, HALF + c0, HALF + c1))
             else:
-                gather(nc, (t, h) in LAG_ON_SCALAR, yl[t, h][:], ywin[t][:], lag_t[:, 32 * h : 32 * h + 32])
+                gather(nc, t % 2 == 0, y_lag[t, h][:], y[t][:], entries(lag_t, HALF * h, HALF * (h + 1)))
 
         def difference(t, h):
-            diff[t, h] = keep.tile([P, HALF], F32, name="diff%d%d" % (t, h), tag="diff%d%d" % (t, h))
-            nc.vector.tensor_tensor(out=diff[t, h][:], in0=ywin[t][:, HALF * h : HALF * (h + 1)], in1=yl[t, h][:], op=ALU.subtract)
+            diff[t, h] = keep.tile([P, HALF], F32, name="diff%d%d" % (t, h))
+            nc.vector.tensor_tensor(
+                out=diff[t, h][:], in0=y[t][:, HALF * h : HALF * (h + 1)], in1=y_lag[t, h][:], op=ALU.subtract
+            )
 
         def square(t, h):
             nc.scalar.activation(
@@ -170,86 +191,105 @@ def tile_picked_yyinwd_log_p_kernel(
             )
 
         def group_sums(t):
-            sums_ps[t] = psum.tile([P, 2 * V], F32, name="sums_ps%d" % t, tag="bank%d" % t)
+            sums_ps[t] = bank_tile("sums_ps%d" % t, t)
             for h in range(2):
                 for d in range(D):
-                    c0 = HALF * h + VH * d
+                    c0 = HALF * h + GROUPS * d
                     nc.tensor.matmul(
-                        out=sums_ps[t][:, VH * h : VH * (h + 1)],
-                        lhsT=sq[t][:, c0 : c0 + VH],
+                        out=sums_ps[t][:, P * h : P * (h + 1)],
+                        lhsT=sq[t][:, c0 : c0 + GROUPS],
                         rhs=ident[:],
                         is_transpose=True,
                         start=(d == 0),
                         stop=(d == D - 1),
                     )
 
-        def logarithms(t):
-            logs = logs_all[:, t, :]
-            nc.scalar.activation(out=logs[:, V:], in_=sums_ps[t][:, :V], func=ACT.Ln, scale=1.0 / D, bias=0.3)
-            nc.scalar.activation(out=logs[:, :V], in_=sums_ps[t][:, :V], func=ACT.Ln, scale=1.0 / D, bias=0.2)
-            if t % 2 == 0:
-                logden_ps[t // 2] = psum.tile([P, 2 * V], F32, name="logden%d" % t, tag="bank%d" % (4 + t // 2))
+        def logarithm(t):
+            turned = logs_turned[:, V * t : V * (t + 1)]
+            nc.scalar.activation(out=turned, in_=sums_ps[t][:, :V], func=ACT.Ln, scale=log_scale, bias=log_bias)
+            if t < 2:
+                log_ps[t] = sums_ps[t][:, V:]
+            elif t == 2:
+                late_logs = bank_tile("late_logs", 4)
+                log_ps[2], log_ps[3] = late_logs[:, :V], late_logs[:, V:]
             for h in range(2):
-                c0 = V * (t % 2) + VH * h
-                nc.tensor.transpose(logden_ps[t // 2][:, c0 : c0 + VH], logs[:, V + VH * h : V + VH * (h + 1)], ident[:])
-            for h in range(2):
-                nc.tensor.transpose(sums_ps[t][:, V + VH * h : V + VH * (h + 1)], logs[:, VH * h : VH * (h + 1)], ident[:])
+                nc.tensor.transpose(log_ps[t][:, GROUPS * h : GROUPS * (h + 1)], turned[:, P * h : P * (h + 1)], ident[:])
 
-        def minima(t):
-            m1 = keep.tile([P, 2, 2 * VH], F32, name="m1_%d" % t)
+        def minimum(t):
+            pairs = keep.tile([P, 2, 2 * GROUPS], F32, name="pairs%d" % t)
             by_half = sq[t][:].rearrange("p (h c) -> p h c", h=2)
-            nc.vector.tensor_tensor(out=m1[:], in0=by_half[:, :, : 2 * VH], in1=by_half[:, :, 2 * VH :], op=ALU.min)
-            m2[t] = keep.tile([P, 2, VH], F32, name="m2_%d" % t)
-            nc.vector.tensor_tensor(out=m2[t][:], in0=m1[:, :, :VH], in1=m1[:, :, VH:], op=ALU.min)
+            nc.vector.tensor_tensor(
+                out=pairs[:], in0=by_half[:, :, : 2 * GROUPS], in1=by_half[:, :, 2 * GROUPS :], op=ALU.min
+            )
+            least[t] = keep.tile([P, 2, GROUPS], F32, name="least%d" % t)
+            nc.vector.tensor_tensor(out=least[t][:], in0=pairs[:, :, :GROUPS], in1=pairs[:, :, GROUPS:], op=ALU.min)
 
         def numerator(t):
             num[t] = keep.tile([P, V], F32, name="num%d" % t)
             nc.vector.scalar_tensor_tensor(
                 out=num[t][:],
-                in0=m2[t][:].rearrange("p h v -> p (h v)"),
-                scalar=unit_t[:, t : t + 1],
-                in1=sums_ps[t][:, V:],
+                in0=least[t][:].rearrange("p h v -> p (h v)"),
+                scalar=unit10[:, t : t + 1],
+                in1=log_ps[t],
                 op0=ALU.mult,
                 op1=ALU.mult,
             )
 
-        for t, h in ((0, 0), (0, 1), (1, 0), (1, 1), (2, 0), (2, 1), (3, 0), (3, 1)):
-            lagged(t, h)
-        for t, h in ((0, 0), (0, 1), (1, 0), (1, 1), (2, 0), (2, 1), (3, 0), (3, 1)):
-            difference(t, h)
-        for t in range(PACK):
-            square(t, 0)
-            square(t, 1)
+        for t in range(2):
+            for h in range(2):
+                lagged(t, h)
+        for h in range(2):
+            difference(0, h)
+        for h in range(2):
+            square(0, h)
+        group_sums(0)
+        for t in range(2, PACK):
+            for h in range(2):
+                lagged(t, h)
+        logarithm(0)
+        for t in range(1, PACK):
+            for h in range(2):
+                difference(t, h)
+        for t in range(1, PACK):
+            for h in range(2):
+                square(t, h)
             group_sums(t)
-        for t in range(PACK):
-            logarithms(t)
-        for t in range(PACK):
-            minima(t)
+        for t in range(1, PACK):
+            logarithm(t)
+        minimum(0)
+        numerator(0)
+        for t in range(1, PACK):
+            minimum(t)
+        for t in range(1, PACK):
             numerator(t)
 
         for t in range(PACK):
-            inv = logs_all[:, 2:, VH * t : VH * (t + 1)]
-            by_half = "p (h v) -> p h v"
-            nc.scalar.activation(
-                out=inv, in_=logden_ps[t // 2][:, V * (t % 2) : V * (t % 2 + 1)].rearrange(by_half, h=2), func=ACT.Exp, scale=-1.0
-            )
-            nc.vector.tensor_tensor(out=sq[t][:, :V].rearrange(by_half, h=2), in0=num[t][:].rearrange(by_half, h=2), in1=inv, op=ALU.mult)
+            inv_t = inv[:, V * t : V * (t + 1)]
+            nc.scalar.activation(out=inv_t, in_=log_ps[t], func=ACT.Sigmoid, scale=-1.0, bias=log_tenth[:])
+            nc.vector.tensor_tensor(out=sq[t][:, :V], in0=num[t][:], in1=inv_t, op=ALU.mult)
 
-        out_banks = (6, 7, 0, 1, 2, 3, 4, 5)
-        r0 = 0
-        for g, width in enumerate(NOTE_CHUNKS):
-            planes = keep.tile([P, PACK, width], BF16, name="planes%d" % g, align_bytes=64)
+        vector_from = (2, PACK, LAST)
+        out_banks = (5, 6, 7, 0, 1, 2)
+        for g, (r0, r1) in enumerate(CHUNKS):
+            width = r1 - r0
+            last_chunk = g == len(CHUNKS) - 1
+            hid_rows = keep.tile([P, PACK, width], BF16, name="hid_rows%d" % g, align_bytes=64)
             for t in range(PACK):
-                gather(nc, (g, t) not in NOTE_ON_VECTOR, planes[:, t, :], sq[t][:], note_t[:, r0 // 16 : (r0 + width) // 16])
+                gather(nc, t >= vector_from[g], hid_rows[:, t, :], sq[t][:], entries(note_t, r0, r1))
             woven = keep.tile([P, width, PACK], BF16, name="woven%d" % g, align_bytes=64)
-            nc.vector.tensor_copy(out=woven[:], in_=planes[:].rearrange("p t r -> p r t"))
+            nc.vector.tensor_copy(
+                out=woven[:].rearrange("p (c i) t -> p c t i", i=4),
+                in_=hid_rows[:].rearrange("p t (c i) -> p c t i", i=4),
+            )
             codes = keep.tile([P, width], U32, name="codes%d" % g, align_bytes=64)
             scales = keep.tile([P, width], U8, name="scales%d" % g, align_bytes=64)
-            nc.vector.quantize_mx(out=codes[:].bitcast(FP8X4), scales=scales[:], in_=woven[:].rearrange("p r t -> p (r t)"))
-            for a in range(2):
-                o_ps = psum.tile([P, 2 * V], F32, name="o_ps%d%d" % (g, a), tag="bank%d" % out_banks[2 * g + a])
+            nc.vector.quantize_mx(
+                out=codes[:].bitcast(FP8X4), scales=scales[:], in_=woven[:].rearrange("p r t -> p (r t)")
+            )
+            for a in range(N // P):
+                out_ps = bank_tile("out_ps%d%d" % (g, a), out_banks[2 * g + a])
                 nc.tensor.matmul_mx(
-                    out=o_ps[:, :width],
+                    out=out_ps[:, :width],
                     lhsT=w2w[:, 2 * P * a : 2 * P * (a + 1)].bitcast(FP4X4),
                     lhsT_scale=w2s[:, P * a : P * (a + 1)],
                     rhs=codes[:].bitcast(FP8X4),
@@ -257,7 +297,7 @@ def tile_picked_yyinwd_log_p_kernel(
                     start=True,
                     stop=True,
                 )
-                o_sb = keep.tile([P, width], F32, name="o_sb%d%d" % (g, a))
-                move(nc, (g, a) in OUT_ON_VECTOR, o_sb[:], o_ps[:, :width])
-                nc.sync.dma_start(out=out[P * a : P * (a + 1), r0 : r0 + width], in_=o_sb[:])
-            r0 += width
+                out_sb = keep.tile([P, width], F32, name="out_sb%d%d" % (g, a))
+                move(nc, last_chunk and a == 1, out_sb[:], out_ps[:, :width])
+                queue = nc.scalar if last_chunk and a == 0 else nc.sync
+                queue.dma_start(out=out[P * a : P * (a + 1), r0:r1], in_=out_sb[:])

from contextlib import ExitStack

import concourse.mybir as mybir
from concourse.masks import make_identity

K, T, S, D, N, H, V, U = 512, 2048, 1024, 4, 256, 512, 256, 512
FLOPS = 2 * K * H * S + 2 * H * N * U

F32 = mybir.dt.float32
BF16 = mybir.dt.bfloat16
I32 = mybir.dt.int32
U32 = mybir.dt.uint32
U16 = mybir.dt.uint16
U8 = mybir.dt.uint8
FP8X4 = mybir.dt.float8_e4m3fn_x4
FP4X4 = mybir.dt.float4_e2m1fn_x4
ACT = mybir.ActivationFunctionType
ALU = mybir.AluOpType

P = 128
PACK = 4
PER_COLUMN = 16
BANK = 512
HALF = S // 2
GROUPS = HALF // D
LAST = PACK - 1

SHORT = 256
PIECES = ((0, SHORT), (SHORT, S - SHORT), (S - SHORT, S))
CHUNKS = ((0, 256), (256, 384), (384, U))


def load_scale_rows(nc, tile, rows):
    for q in range(4):
        nc.sync.dma_start(
            out=tile[32 * q : 32 * q + 32, :].bitcast(I32),
            in_=rows[4 * q : 4 * q + 4, :].bitcast(I32).partition_broadcast(8),
        )


def entries(list_tile, first, end):
    return list_tile[:, first // PER_COLUMN : end // PER_COLUMN]


def gather(nc, on_vector, out, window, offsets):
    if on_vector:
        nc.vector.tensor_copy(out=out, in_=window.indirect(offsets))
    else:
        nc.scalar.activation(out=out, in_=window.indirect(offsets), func=ACT.Copy)


def move(nc, on_vector, out, in_):
    if on_vector:
        nc.vector.tensor_copy(out=out, in_=in_)
    else:
        nc.scalar.copy(out=out, in_=in_)


def tile_picked_yyinwd_log_p_kernel(
    tc, x_words, x_scales, w1_words, w1_scales, unit, w2_words, w2_scales, offs, lag, note, out
):
    nc = tc.nc
    with ExitStack() as ctx:
        lists = ctx.enter_context(tc.tile_pool(name="lists", bufs=1))
        keep = ctx.enter_context(tc.tile_pool(name="keep", bufs=1))
        psum = ctx.enter_context(tc.psum_pool(name="psum", bufs=1))

        def bank_tile(name, bank):
            return psum.tile([P, BANK], F32, name=name, tag="bank%d" % bank)

        offs_t = lists.tile([P, S // PER_COLUMN], U16, name="offs_t")
        lag_t = lists.tile([P, S // PER_COLUMN], U16, name="lag_t")
        note_t = lists.tile([P, U // PER_COLUMN], U16, name="note_t")

        xw = keep.tile([P, T], U32, name="xw", align_bytes=64)
        xs = keep.tile([P, T], U8, name="xs", align_bytes=64)
        w1w_raw = keep.tile([P, 2 * H], U8, name="w1w_raw", align_bytes=64)
        w1s_raw = keep.tile([P, H], U8, name="w1s_raw", tag="w1s_then_words", align_bytes=64)
        w1w = keep.tile([P, 2 * H], U8, name="w1w", align_bytes=64)
        w1s = keep.tile([P, H], U8, name="w1s", align_bytes=64)
        w2w = keep.tile([P, 2 * N], U8, name="w2w", align_bytes=64)
        w2s = keep.tile([P, N], U8, name="w2s", align_bytes=64)
        unit_t = keep.tile([P, PACK], F32, name="unit_t")
        ident = keep.tile([P, P], F32, name="ident")

        make_identity(nc, ident[:])
        nc.sync.dma_start(offs_t[:], offs)
        load_scale_rows(nc, xs, x_scales[0])
        nc.sync.dma_start(out=xw[:].bitcast(I32), in_=x_words[0].rearrange("p n t -> p (n t)").bitcast(I32))
        load_scale_rows(nc, w1s_raw, w1_scales[0])
        nc.sync.dma_start(out=w1w_raw[:].bitcast(I32), in_=w1_words[0].bitcast(I32))
        nc.sync.dma_start(lag_t[:], lag)
        nc.sync.dma_start(note_t[:], note)
        nc.sync.dma_start(out=unit_t[:], in_=unit.rearrange("(p t) o -> p (t o)", t=PACK))
        nc.sync.dma_start(out=w2w[:].bitcast(I32), in_=w2_words[0].bitcast(I32))
        load_scale_rows(nc, w2s, w2_scales[0])

        one = keep.tile([P, 1], F32, name="one")
        log_tenth = keep.tile([P, 1], F32, name="log_tenth")
        nc.vector.memset(one[:], 1.0)
        nc.scalar.activation(out=log_tenth[:], in_=one[:], func=ACT.Ln, scale=0.1)

        nc.scalar.copy(
            out=w1w[:].bitcast(U16).rearrange("p (t m) -> p t m", t=PACK),
            in_=w1w_raw[:].bitcast(U16).rearrange("p (m t) -> p t m", t=PACK),
        )
        nc.vector.tensor_copy(
            out=w1s[:].rearrange("p (t m) -> p t m", t=PACK), in_=w1s_raw[:].rearrange("p (m t) -> p t m", t=PACK)
        )

        xq_s = keep.tile([P, S], U8, name="xq_s", align_bytes=64)
        nc.vector.tensor_copy(out=xq_s[:], in_=xs[:].indirect(offs_t[:]))
        xq_w = keep.tile([P, S], U32, name="xq_w", tag="w1s_then_words", align_bytes=64)
        for c0, c1 in PIECES:
            nc.vector.tensor_copy(out=xq_w[:, c0:c1], in_=xw[:].indirect(entries(offs_t, c0, c1)))

        y = [keep.tile([P, S], F32, name="y%d" % t) for t in range(PACK)]
        sq = [keep.tile([P, S], F32, name="sq%d" % t) for t in range(PACK)]
        y_banks = [bank_tile("y_bank%d" % b, b) for b in range(8)]
        y_ps = {}

        def product(t, k, bank, column):
            c0, c1 = PIECES[k]
            y_ps[t, k] = y_banks[bank][:, column : column + c1 - c0]
            nc.tensor.matmul_mx(
                out=y_ps[t, k],
                lhsT=w1w[:, 2 * P * t : 2 * P * (t + 1)].bitcast(FP4X4),
                lhsT_scale=w1s[:, P * t : P * (t + 1)],
                rhs=xq_w[:, c0:c1].bitcast(FP8X4),
                rhs_scale=xq_s[:, c0:c1],
                start=True,
                stop=True,
            )

        def empty_bank(t, k):
            c0, c1 = PIECES[k]
            move(nc, t == 1 and k > 0, y[t][:, c0:c1], y_ps[t, k])

        for t in range(PACK):
            product(t, 0, t // 2, SHORT * (t % 2))
        for k, first_bank in ((1, 2), (2, 6)):
            for t in range(2):
                product(t, k, first_bank + t, 0)
        for t in range(PACK):
            empty_bank(t, 0)
        for t in range(2):
            empty_bank(t, 1)
            empty_bank(t, 2)
        for t in range(2, PACK):
            product(t, 1, 2 + t, 0)
            product(t, 2, 4 + t, SHORT)
            empty_bank(t, 1)
            empty_bank(t, 2)

        logs_turned = keep.tile([P, PACK * V], F32, name="logs_turned")
        inv = keep.tile([P, PACK * V], F32, name="inv")
        log_bias = inv[:, 0:1]
        log_scale = inv[:, V : V + 1]
        nc.vector.tensor_scalar(out=log_bias, in0=ident[:, 0:1], scalar1=0.0, scalar2=0.2, op0=ALU.mult, op1=ALU.add)
        nc.vector.memset(log_scale, 1.0 / D)
        unit10 = keep.tile([P, PACK], F32, name="unit10")
        nc.vector.tensor_scalar(out=unit10[:], in0=unit_t[:], scalar1=10.0, scalar2=None, op0=ALU.mult)

        y_lag = {}
        diff = {}
        sums_ps = {}
        log_ps = {}
        least = {}
        num = {}

        def lagged(t, h):
            y_lag[t, h] = keep.tile([P, HALF], F32, name="y_lag%d%d" % (t, h))
            if (t, h) == (LAST, 1):
                for c0 in (0, HALF // 2):
                    c1 = c0 + HALF // 2
                    gather(nc, c0 == 0, y_lag[t, h][:, c0:c1], y[t][:], entries(lag_t, HALF + c0, HALF + c1))
            else:
                gather(nc, t % 2 == 0, y_lag[t, h][:], y[t][:], entries(lag_t, HALF * h, HALF * (h + 1)))

        def difference(t, h):
            diff[t, h] = keep.tile([P, HALF], F32, name="diff%d%d" % (t, h))
            nc.vector.tensor_tensor(
                out=diff[t, h][:], in0=y[t][:, HALF * h : HALF * (h + 1)], in1=y_lag[t, h][:], op=ALU.subtract
            )

        def square(t, h):
            nc.scalar.activation(
                out=sq[t][:, HALF * h : HALF * (h + 1)].rearrange("p (d v) -> p v d", d=D),
                in_=diff[t, h][:].rearrange("p (v d) -> p v d", d=D),
                func=ACT.Square,
            )

        def group_sums(t):
            sums_ps[t] = bank_tile("sums_ps%d" % t, t)
            for h in range(2):
                for d in range(D):
                    c0 = HALF * h + GROUPS * d
                    nc.tensor.matmul(
                        out=sums_ps[t][:, P * h : P * (h + 1)],
                        lhsT=sq[t][:, c0 : c0 + GROUPS],
                        rhs=ident[:],
                        is_transpose=True,
                        start=(d == 0),
                        stop=(d == D - 1),
                    )

        def logarithm(t):
            turned = logs_turned[:, V * t : V * (t + 1)]
            nc.scalar.activation(out=turned, in_=sums_ps[t][:, :V], func=ACT.Ln, scale=log_scale, bias=log_bias)
            if t < 2:
                log_ps[t] = sums_ps[t][:, V:]
            elif t == 2:
                late_logs = bank_tile("late_logs", 4)
                log_ps[2], log_ps[3] = late_logs[:, :V], late_logs[:, V:]
            for h in range(2):
                nc.tensor.transpose(log_ps[t][:, GROUPS * h : GROUPS * (h + 1)], turned[:, P * h : P * (h + 1)], ident[:])

        def minimum(t):
            pairs = keep.tile([P, 2, 2 * GROUPS], F32, name="pairs%d" % t)
            by_half = sq[t][:].rearrange("p (h c) -> p h c", h=2)
            nc.vector.tensor_tensor(
                out=pairs[:], in0=by_half[:, :, : 2 * GROUPS], in1=by_half[:, :, 2 * GROUPS :], op=ALU.min
            )
            least[t] = keep.tile([P, 2, GROUPS], F32, name="least%d" % t)
            nc.vector.tensor_tensor(out=least[t][:], in0=pairs[:, :, :GROUPS], in1=pairs[:, :, GROUPS:], op=ALU.min)

        def numerator(t):
            num[t] = keep.tile([P, V], F32, name="num%d" % t)
            nc.vector.scalar_tensor_tensor(
                out=num[t][:],
                in0=least[t][:].rearrange("p h v -> p (h v)"),
                scalar=unit10[:, t : t + 1],
                in1=log_ps[t],
                op0=ALU.mult,
                op1=ALU.mult,
            )

        for t in range(2):
            for h in range(2):
                lagged(t, h)
        for h in range(2):
            difference(0, h)
        for h in range(2):
            square(0, h)
        group_sums(0)
        for t in range(2, PACK):
            for h in range(2):
                lagged(t, h)
        logarithm(0)
        for t in range(1, PACK):
            for h in range(2):
                difference(t, h)
        for t in range(1, PACK):
            for h in range(2):
                square(t, h)
            group_sums(t)
        for t in range(1, PACK):
            logarithm(t)
        minimum(0)
        numerator(0)
        for t in range(1, PACK):
            minimum(t)
        for t in range(1, PACK):
            numerator(t)

        for t in range(PACK):
            inv_t = inv[:, V * t : V * (t + 1)]
            nc.scalar.activation(out=inv_t, in_=log_ps[t], func=ACT.Sigmoid, scale=-1.0, bias=log_tenth[:])
            nc.vector.tensor_tensor(out=sq[t][:, :V], in0=num[t][:], in1=inv_t, op=ALU.mult)

        vector_from = (2, PACK, LAST)
        out_banks = (5, 6, 7, 0, 1, 2)
        for g, (r0, r1) in enumerate(CHUNKS):
            width = r1 - r0
            last_chunk = g == len(CHUNKS) - 1
            hid_rows = keep.tile([P, PACK, width], BF16, name="hid_rows%d" % g, align_bytes=64)
            for t in range(PACK):
                gather(nc, t >= vector_from[g], hid_rows[:, t, :], sq[t][:], entries(note_t, r0, r1))
            woven = keep.tile([P, width, PACK], BF16, name="woven%d" % g, align_bytes=64)
            nc.vector.tensor_copy(
                out=woven[:].rearrange("p (c i) t -> p c t i", i=4),
                in_=hid_rows[:].rearrange("p t (c i) -> p c t i", i=4),
            )
            codes = keep.tile([P, width], U32, name="codes%d" % g, align_bytes=64)
            scales = keep.tile([P, width], U8, name="scales%d" % g, align_bytes=64)
            nc.vector.quantize_mx(
                out=codes[:].bitcast(FP8X4), scales=scales[:], in_=woven[:].rearrange("p r t -> p (r t)")
            )
            for a in range(N // P):
                out_ps = bank_tile("out_ps%d%d" % (g, a), out_banks[2 * g + a])
                nc.tensor.matmul_mx(
                    out=out_ps[:, :width],
                    lhsT=w2w[:, 2 * P * a : 2 * P * (a + 1)].bitcast(FP4X4),
                    lhsT_scale=w2s[:, P * a : P * (a + 1)],
                    rhs=codes[:].bitcast(FP8X4),
                    rhs_scale=scales[:],
                    start=True,
                    stop=True,
                )
                out_sb = keep.tile([P, width], F32, name="out_sb%d%d" % (g, a))
                move(nc, last_chunk and a == 1, out_sb[:], out_ps[:, :width])
                queue = nc.scalar if last_chunk and a == 0 else nc.sync
                queue.dma_start(out=out[P * a : P * (a + 1), r0:r1], in_=out_sb[:])
